import numpy as np
import ml_dtypes


def mxq(x, axis, fmt="e4m3"):
    dtype, down = {"e4m3": (ml_dtypes.float8_e4m3fn, 7), "e5m2": (ml_dtypes.float8_e5m2, 14)}[fmt]
    v = np.moveaxis(np.asarray(x, np.float32).astype(ml_dtypes.bfloat16).astype(np.float64), axis, -1)
    blocks = v.reshape(v.shape[:-1] + (-1, 32))
    amax = np.abs(blocks).max(-1, keepdims=True)
    byte = np.maximum(np.where(amax > 0, np.frexp(amax)[1] - 1 + 127, 0) - down, 1)
    scale = np.exp2(byte - 127.0)
    codes = (blocks / scale).astype(np.float32).astype(dtype).astype(np.float64)
    return np.moveaxis((codes * scale).reshape(v.shape), -1, axis)


WIDE = False


def mx_kscale(k):
    if not WIDE:
        return np.ones(k)
    levels = np.array([10, -10, 5, -5, 0])
    if k % 512:
        return np.exp2(np.random.permutation(np.resize(levels, k // 32))).repeat(32)
    a = np.empty((k // 512, 16))
    for p in range(k // 512):
        a[p, :8] = np.random.permutation(np.resize(levels, 8))
        for g in range(8):
            far = levels[np.abs(levels - a[p, g]) >= 10]
            a[p, g + 8] = far[np.random.randint(len(far))]
    return np.exp2(a.ravel()).repeat(32)


def f64(x):
    return np.asarray(x).astype(np.float64)


E2M1 = np.array([0.0, 0.5, 1.0, 1.5, 2.0, 3.0, 4.0, 6.0, -0.0, -0.5, -1.0, -1.5, -2.0, -3.0, -4.0, -6.0])


def pack_weight(w, fmt):
    k, n = w.shape
    w = f64(np.asarray(w, np.float32).astype(ml_dtypes.bfloat16)).reshape(k // 32, 32, n)
    amax = np.abs(w).max(1)
    if fmt == "e4m3":
        byte = np.frexp(amax)[1] - 1 + 127 - 7
    else:
        mant, ex = np.frexp(amax / 6.0)
        byte = np.where(mant > 0.5, ex, ex - 1) + 127
    byte = np.clip(np.where(amax > 0, byte, 1), 1, 254)
    scaled = (w * np.exp2(127.0 - byte)[:, None, :]).reshape(k, n).astype(np.float32)
    by_word = np.ascontiguousarray(scaled.reshape(k // 512, 128, 4, n).transpose(0, 1, 3, 2))
    if fmt == "e4m3":
        words = by_word.astype(ml_dtypes.float8_e4m3fn).view(np.uint8)
    else:
        c = by_word.astype(ml_dtypes.float4_e2m1fn).view(np.uint8) & 0xF
        words = (c[..., 0::2] | (c[..., 1::2] << 4)).reshape(k // 512, 128, 2 * n)
    return np.ascontiguousarray(words), np.ascontiguousarray(byte.astype(np.uint8).reshape(k // 512, 16, n))


def unpack_weight(words, scales, fmt):
    g, _, n = scales.shape
    words = np.ascontiguousarray(words).reshape(g, 128, n, -1)
    if fmt == "e4m3":
        vals = words.view(ml_dtypes.float8_e4m3fn).astype(np.float64)
    else:
        nib = np.empty((g, 128, n, 4), np.uint8)
        nib[..., 0::2] = words & 0xF
        nib[..., 1::2] = words >> 4
        vals = E2M1[nib]
    vals = vals * np.repeat(np.exp2(scales.astype(np.float64) - 127.0), 8, axis=1)[..., None]
    return vals.transpose(0, 1, 3, 2).reshape(g * 512, n)


K, R, M, T = 2048, 512, 1536, 512


def setup_inputs():
    n = np.random.standard_normal
    s = mx_kscale(K)[:, None]
    u = mx_kscale(R)[:, None]
    p_w4 = pack_weight(n((K, M)) / np.sqrt(K) / s, "e2m1")
    return {
        "x": (n((K, T)) * s).astype(np.float32),
        "w4_words": p_w4[0],
        "w4_scales": p_w4[1],
        "down": (n((K, R)) / np.sqrt(K) / s * u.T).astype(np.float32),
        "up": (0.5 * n((R, M)) / np.sqrt(R) / u).astype(np.float32),
        "b": (0.3 * n(1536)).astype(np.float32),
    }


def reference(x, w4_words, w4_scales, down, up, b):
    x_ = mxq(f64(x), 0, "e4m3")
    w4_ = unpack_weight(w4_words, w4_scales, "e2m1")
    down_ = mxq(f64(down), 0, "e4m3")
    up_ = mxq(f64(up), 0, "e4m3")
    h_ = mxq(down_.T @ x_, 0, "e4m3")
    y = w4_.T @ x_ + up_.T @ h_
    return y + f64(b)[:, None]

@@ -1,0 +1,248 @@
+from contextlib import ExitStack
+
+import concourse.mybir as mybir
+from concourse.masks import make_identity
+
+K, R, N, T = 2048, 512, 1536, 512
+FLOPS = 2 * T * (K * R + K * N + R * N)
+
+F32 = mybir.dt.float32
+BF16 = mybir.dt.bfloat16
+I32 = mybir.dt.int32
+U32 = mybir.dt.uint32
+U8 = mybir.dt.uint8
+E4M3X4 = mybir.dt.float8_e4m3fn_x4
+E2M1X4 = mybir.dt.float4_e2m1fn_x4
+IDENTITY = mybir.ActivationFunctionType.Identity
+ADD = mybir.AluOpType.add
+
+P = 128
+PACK = 4
+K_PASS = P * PACK
+PASSES = K // K_PASS
+THIRDS = 3
+COLS = N // THIRDS
+TILES = COLS // P
+N_TILES = N // P
+
+X_SPLIT = 352
+DOWN_SPLIT = 88
+UP_SPLIT = 384
+H_SPLIT = 352
+
+
+def tile_mix_lowrank_fm_bias_kernel(tc, x, w4_words, w4_scales, down, up, b, out):
+    nc = tc.nc
+    with ExitStack() as ctx:
+        keep = ctx.enter_context(tc.tile_pool(name="keep", bufs=1))
+        psum = ctx.enter_context(tc.psum_pool(name="psum", bufs=1))
+        ctx.enter_context(tc.manual_schedule())
+
+        def sbuf(name, shape, dtype):
+            return keep.tile(shape, dtype, name=name, align_bytes=64)
+
+        def bank(i, name):
+            return psum.tile([P, T], F32, name=name, tag=f"bank{i}")
+
+        x_raw = [sbuf(f"x_raw{g}", [P, PACK, T], F32) for g in range(PASSES)]
+        x_bf = [sbuf(f"x_bf{g}", [P, T, PACK], BF16) for g in range(PASSES)]
+        x_codes = [sbuf(f"x_codes{g}", [P, T], U32) for g in range(PASSES)]
+        x_scales = [sbuf(f"x_scales{g}", [P, T], U8) for g in range(PASSES)]
+        d_raw = [sbuf(f"d_raw{g}", [P, PACK, R], F32) for g in range(PASSES)]
+        d_bf = [sbuf(f"d_bf{g}", [P, PACK, P, PACK], BF16) for g in range(PASSES)]
+        d_codes = [sbuf(f"d_codes{g}", [P, R], U32) for g in range(PASSES)]
+        d_scales = [sbuf(f"d_scales{g}", [P, R], U8) for g in range(PASSES)]
+        u_raw = [sbuf(f"u_raw{c}", [P, PACK, COLS], F32) for c in range(THIRDS)]
+        u_bf = [sbuf(f"u_bf{c}", [P, COLS, PACK], BF16) for c in range(THIRDS)]
+        u_codes = [sbuf(f"u_codes{c}", [P, COLS], U32) for c in range(THIRDS)]
+        u_scales = [sbuf(f"u_scales{c}", [P, COLS], U8) for c in range(THIRDS)]
+        w_words = [sbuf(f"w_words{c}", [P, PASSES, 2 * COLS], U8) for c in range(THIRDS)]
+        w_scales = [sbuf(f"w_scales{c}", [P, PASSES, COLS], U8) for c in range(THIRDS)]
+        h_sb = sbuf("h_sb", [P, PACK, T], BF16)
+        h_bf = sbuf("h_bf", [P, T, PACK], BF16)
+        h_codes = sbuf("h_codes", [P, T], U32)
+        h_scales = sbuf("h_scales", [P, T], U8)
+        ident = sbuf("ident", [P, P], F32)
+        b_rows = sbuf("b_rows", [P, P], F32)
+        b_cols = sbuf("b_cols", [P, N_TILES], F32)
+        warm = sbuf("warm", [P, 1], F32)
+        y_sb = [sbuf(f"y_sb{i}", [P, T], F32) for i in range(N_TILES)]
+
+        nc.vector.memset(warm[:], 0.0)
+        nc.vector.memset(b_rows[:], 0.0)
+        for c in range(THIRDS):
+            nc.vector.memset(w_scales[c][:].rearrange("p g n -> p (g n)").bitcast(I32), 0)
+        make_identity(nc, ident[:])
+
+        def load_rows(tile, rows):
+            nc.sync.dma_start(out=tile[:], in_=rows.rearrange("(p j) w -> p j w", j=PACK))
+
+        def load_w4(c):
+            cols = slice(c * COLS, (c + 1) * COLS)
+            nc.sync.dma_start(
+                out=w_words[c][:],
+                in_=w4_words[:, :, 2 * c * COLS : 2 * (c + 1) * COLS].rearrange("g p n -> p g n"),
+            )
+            for r in range(4):
+                nc.sync.dma_start(
+                    out=w_scales[c][r:P:32, :, :].bitcast(I32),
+                    in_=w4_scales[:, r:16:4, cols].rearrange("g q n -> q g n").bitcast(I32),
+                )
+
+        nc.scalar.dma_start(out=b_rows[0:N_TILES, :], in_=b.rearrange("(c p) -> c p", p=P))
+        k_rows = [slice(g * K_PASS, (g + 1) * K_PASS) for g in range(PASSES)]
+        u_cols = [slice(c * COLS, (c + 1) * COLS) for c in range(THIRDS)]
+        load_rows(x_raw[0], x[k_rows[0], :])
+        load_rows(d_raw[0], down[k_rows[0], :])
+        load_w4(0)
+        for g in range(1, PASSES):
+            load_rows(x_raw[g], x[k_rows[g], :])
+            load_rows(d_raw[g], down[k_rows[g], :])
+        load_w4(1)
+        load_rows(u_raw[0], up[:, u_cols[0]])
+        load_w4(2)
+        load_rows(u_raw[1], up[:, u_cols[1]])
+        load_rows(u_raw[2], up[:, u_cols[2]])
+
+        def interleave(copy, dst, src, lo, hi):
+            copy(
+                out=dst[:, lo:hi, :].rearrange("p (c i) t -> p c t i", i=4),
+                in_=src[:, :, lo:hi].rearrange("p t (c i) -> p c t i", i=4),
+            )
+
+        def interleave_both(dst, src, split, width):
+            interleave(nc.vector.tensor_copy, dst, src, 0, split)
+            interleave(nc.scalar.copy, dst, src, split, width)
+
+        def permute(copy, g, lo, hi):
+            copy(
+                out=d_bf[g][:, :, lo:hi, :].rearrange("p t m j -> p m j t"),
+                in_=d_raw[g][:, :, 4 * lo : 4 * hi].rearrange("p j (m t) -> p m j t", t=4),
+            )
+
+        def permute_both(g):
+            permute(nc.vector.tensor_copy, g, 0, DOWN_SPLIT)
+            permute(nc.scalar.copy, g, DOWN_SPLIT, P)
+
+        def quantize(codes, scales, grouped):
+            nc.vector.quantize_mx(out=codes.bitcast(E4M3X4), scales=scales, in_=grouped)
+
+        def quantize_rows(codes, scales, grouped):
+            quantize(codes[:], scales[:], grouped[:].rearrange("p w j -> p (w j)"))
+
+        def w4_pass(i, acc, g):
+            c, m = i // TILES, (i % TILES) * P
+            nc.tensor.matmul_mx(
+                out=acc[:],
+                lhsT=w_words[c][:, g, 2 * m : 2 * (m + P)].bitcast(E2M1X4),
+                lhsT_scale=w_scales[c][:, g, m : m + P],
+                rhs=x_codes[g][:].bitcast(E4M3X4),
+                rhs_scale=x_scales[g][:],
+                start=(g == 0),
+                stop=False,
+            )
+
+        def up_pass(i, acc):
+            c, m = i // TILES, (i % TILES) * P
+            nc.tensor.matmul_mx(
+                out=acc[:],
+                lhsT=u_codes[c][:, m : m + P].bitcast(E4M3X4),
+                lhsT_scale=u_scales[c][:, m : m + P],
+                rhs=h_codes[:].bitcast(E4M3X4),
+                rhs_scale=h_scales[:],
+                start=False,
+                stop=True,
+            )
+
+        def h_pass(j, acc, g):
+            cols = slice(j * P, (j + 1) * P)
+            nc.tensor.matmul_mx(
+                out=acc[:],
+                lhsT=d_codes[g][:, cols].bitcast(E4M3X4),
+                lhsT_scale=d_scales[g][:, cols],
+                rhs=x_codes[g][:].bitcast(E4M3X4),
+                rhs_scale=x_scales[g][:],
+                start=(g == 0),
+                stop=(g == PASSES - 1),
+            )
+
+        def finish(i, acc, on_vector):
+            bias = b_cols[:, i : i + 1]
+            if on_vector:
+                nc.vector.tensor_scalar(out=y_sb[i][:], in0=acc[:], scalar1=bias, scalar2=None, op0=ADD)
+            else:
+                nc.scalar.activation(out=y_sb[i][:], in_=acc[:], func=IDENTITY, bias=bias)
+            nc.sync.dma_start(out=out[i * P : (i + 1) * P, :], in_=y_sb[i][:])
+
+        nc.scalar.activation(out=warm[:], in_=warm[:], func=IDENTITY)
+        b_psum = bank(7, "b_psum")
+        nc.tensor.transpose(b_psum[:, 0:P], b_rows[:], ident[:])
+
+        acc = {}
+        h_acc = [bank(j, f"h{j}") for j in range(PACK)]
+
+        for g in range(PASSES):
+            interleave_both(x_bf[g], x_raw[g], X_SPLIT, T)
+            if g == 0:
+                nc.scalar.copy(out=b_cols[:], in_=b_psum[:, 0:N_TILES])
+                for i in range(TILES):
+                    acc[i] = bank(4 + i, f"y{i}")
+            else:
+                quantize(d_codes[g - 1][:], d_scales[g - 1][:], d_bf[g - 1][:].rearrange("p t m j -> p (t m j)"))
+                for j in range(PACK):
+                    h_pass(j, h_acc[j], g - 1)
+            quantize_rows(x_codes[g], x_scales[g], x_bf[g])
+            for i in range(TILES):
+                w4_pass(i, acc[i], g)
+            permute_both(g)
+
+        last = PASSES - 1
+        for j in range(PACK):
+            cols = slice(j * P, (j + 1) * P)
+            quantize(d_codes[last][:, cols], d_scales[last][:, cols], d_bf[last][:, j, :, :].rearrange("p m j -> p (m j)"))
+        for j in range(PACK):
+            h_pass(j, h_acc[j], last)
+        for j in range(PACK):
+            copy = nc.vector.tensor_copy if j % 2 else nc.scalar.copy
+            copy(out=h_sb[:, j, :], in_=h_acc[j][:])
+        interleave_both(h_bf, h_sb, H_SPLIT, T)
+        quantize_rows(h_codes, h_scales, h_bf)
+        interleave_both(u_bf[0], u_raw[0], UP_SPLIT, COLS)
+        quantize_rows(u_codes[0], u_scales[0], u_bf[0])
+
+        def w4_tile(i):
+            acc[i] = bank(i - 4, f"y{i}")
+            for g in range(PASSES):
+                w4_pass(i, acc[i], g)
+
+        for i in (4, 5, 6):
+            w4_tile(i)
+        for i in range(4):
+            up_pass(i, acc[i])
+        w4_tile(7)
+        finish(0, acc[0], False)
+        finish(1, acc[1], False)
+        interleave_both(u_bf[1], u_raw[1], UP_SPLIT, COLS)
+        finish(2, acc[2], False)
+        finish(3, acc[3], True)
+        quantize_rows(u_codes[1], u_scales[1], u_bf[1])
+        w4_tile(8)
+        for i in range(4, 8):
+            up_pass(i, acc[i])
+        finish(4, acc[4], False)
+        w4_tile(9)
+        finish(5, acc[5], False)
+        interleave_both(u_bf[2], u_raw[2], UP_SPLIT, COLS)
+        w4_tile(10)
+        finish(6, acc[6], False)
+        finish(7, acc[7], True)
+        quantize_rows(u_codes[2], u_scales[2], u_bf[2])
+        up_pass(8, acc[8])
+        finish(8, acc[8], False)
+        up_pass(9, acc[9])
+        finish(9, acc[9], True)
+        w4_tile(11)
+        up_pass(10, acc[10])
+        finish(10, acc[10], False)
+        up_pass(11, acc[11])
+        finish(11, acc[11], True)

@@ -20,10 +20,12 @@ P = 128
 PACK = 4
 K_PASS = P * PACK
 PASSES = K // K_PASS
-THIRDS = 3
-COLS = N // THIRDS
-TILES = COLS // P
 N_TILES = N // P
+W_COLS = (512, 1024)
+W_LOADS = 3
+U_LOADS = 2
+WL = N // W_LOADS
+UL = N // U_LOADS
 
 X_SPLIT = 352
 DOWN_SPLIT = 88
@@ -52,12 +54,12 @@ def tile_mix_lowrank_fm_bias_kernel(tc, x, w4_words, w4_scales, down, up, b, out
         d_bf = [sbuf(f"d_bf{g}", [P, PACK, P, PACK], BF16) for g in range(PASSES)]
         d_codes = [sbuf(f"d_codes{g}", [P, R], U32) for g in range(PASSES)]
         d_scales = [sbuf(f"d_scales{g}", [P, R], U8) for g in range(PASSES)]
-        u_raw = [sbuf(f"u_raw{c}", [P, PACK, COLS], F32) for c in range(THIRDS)]
-        u_bf = [sbuf(f"u_bf{c}", [P, COLS, PACK], BF16) for c in range(THIRDS)]
-        u_codes = [sbuf(f"u_codes{c}", [P, COLS], U32) for c in range(THIRDS)]
-        u_scales = [sbuf(f"u_scales{c}", [P, COLS], U8) for c in range(THIRDS)]
-        w_words = [sbuf(f"w_words{c}", [P, PASSES, 2 * COLS], U8) for c in range(THIRDS)]
-        w_scales = [sbuf(f"w_scales{c}", [P, PASSES, COLS], U8) for c in range(THIRDS)]
+        u_raw = [sbuf(f"u_raw{c}", [P, PACK, UL], F32) for c in range(U_LOADS)]
+        u_bf = [sbuf(f"u_bf{c}", [P, UL, PACK], BF16) for c in range(U_LOADS)]
+        u_codes = [sbuf(f"u_codes{c}", [P, UL], U32) for c in range(U_LOADS)]
+        u_scales = [sbuf(f"u_scales{c}", [P, UL], U8) for c in range(U_LOADS)]
+        w_words = [sbuf(f"w_words{c}", [P, PASSES, 2 * WL], U8) for c in range(W_LOADS)]
+        w_scales = [sbuf(f"w_scales{c}", [P, PASSES, n], U8) for c, n in enumerate(W_COLS)]
         h_sb = sbuf("h_sb", [P, PACK, T], BF16)
         h_bf = sbuf("h_bf", [P, T, PACK], BF16)
         h_codes = sbuf("h_codes", [P, T], U32)
@@ -70,19 +72,21 @@ def tile_mix_lowrank_fm_bias_kernel(tc, x, w4_words, w4_scales, down, up, b, out
 
         nc.vector.memset(warm[:], 0.0)
         nc.vector.memset(b_rows[:], 0.0)
-        for c in range(THIRDS):
+        for c in range(2):
             nc.vector.memset(w_scales[c][:].rearrange("p g n -> p (g n)").bitcast(I32), 0)
         make_identity(nc, ident[:])
 
         def load_rows(tile, rows):
             nc.sync.dma_start(out=tile[:], in_=rows.rearrange("(p j) w -> p j w", j=PACK))
 
-        def load_w4(c):
-            cols = slice(c * COLS, (c + 1) * COLS)
+        def load_w_words(c):
             nc.sync.dma_start(
                 out=w_words[c][:],
-                in_=w4_words[:, :, 2 * c * COLS : 2 * (c + 1) * COLS].rearrange("g p n -> p g n"),
+                in_=w4_words[:, :, 2 * c * WL : 2 * (c + 1) * WL].rearrange("g p n -> p g n"),
             )
+
+        def load_w_scales(c):
+            cols = slice(sum(W_COLS[:c]), sum(W_COLS[: c + 1]))
             for r in range(4):
                 nc.sync.dma_start(
                     out=w_scales[c][r:P:32, :, :].bitcast(I32),
@@ -91,18 +95,19 @@ def tile_mix_lowrank_fm_bias_kernel(tc, x, w4_words, w4_scales, down, up, b, out
 
         nc.scalar.dma_start(out=b_rows[0:N_TILES, :], in_=b.rearrange("(c p) -> c p", p=P))
         k_rows = [slice(g * K_PASS, (g + 1) * K_PASS) for g in range(PASSES)]
-        u_cols = [slice(c * COLS, (c + 1) * COLS) for c in range(THIRDS)]
+        u_cols = [slice(c * UL, (c + 1) * UL) for c in range(U_LOADS)]
         load_rows(x_raw[0], x[k_rows[0], :])
         load_rows(d_raw[0], down[k_rows[0], :])
-        load_w4(0)
+        load_w_words(0)
+        load_w_scales(0)
         for g in range(1, PASSES):
             load_rows(x_raw[g], x[k_rows[g], :])
             load_rows(d_raw[g], down[k_rows[g], :])
-        load_w4(1)
+        load_w_words(1)
+        load_w_scales(1)
         load_rows(u_raw[0], up[:, u_cols[0]])
-        load_w4(2)
+        load_w_words(2)
         load_rows(u_raw[1], up[:, u_cols[1]])
-        load_rows(u_raw[2], up[:, u_cols[2]])
 
         def interleave(copy, dst, src, lo, hi):
             copy(
@@ -115,10 +120,11 @@ def tile_mix_lowrank_fm_bias_kernel(tc, x, w4_words, w4_scales, down, up, b, out
             interleave(nc.scalar.copy, dst, src, split, width)
 
         def permute(copy, g, lo, hi):
-            copy(
-                out=d_bf[g][:, :, lo:hi, :].rearrange("p t m j -> p m j t"),
-                in_=d_raw[g][:, :, 4 * lo : 4 * hi].rearrange("p j (m t) -> p m j t", t=4),
-            )
+            for t in (0, 2):
+                copy(
+                    out=d_bf[g][:, t : t + 2, lo:hi, :].rearrange("p t m j -> p m j t"),
+                    in_=d_raw[g][:, :, 4 * lo : 4 * hi].rearrange("p j (m t) -> p m j t", t=4)[:, :, :, t : t + 2],
+                )
 
         def permute_both(g):
             permute(nc.vector.tensor_copy, g, 0, DOWN_SPLIT)
@@ -131,11 +137,12 @@ def tile_mix_lowrank_fm_bias_kernel(tc, x, w4_words, w4_scales, down, up, b, out
             quantize(codes[:], scales[:], grouped[:].rearrange("p w j -> p (w j)"))
 
         def w4_pass(i, acc, g):
-            c, m = i // TILES, (i % TILES) * P
+            c, m = i * P // WL, i * P % WL
+            d, n = (0, i * P) if i * P < W_COLS[0] else (1, i * P - W_COLS[0])
             nc.tensor.matmul_mx(
-                out=acc[:],
+                out=acc,
                 lhsT=w_words[c][:, g, 2 * m : 2 * (m + P)].bitcast(E2M1X4),
-                lhsT_scale=w_scales[c][:, g, m : m + P],
+                lhsT_scale=w_scales[d][:, g, n : n + P],
                 rhs=x_codes[g][:].bitcast(E4M3X4),
                 rhs_scale=x_scales[g][:],
                 start=(g == 0),
@@ -143,9 +150,9 @@ def tile_mix_lowrank_fm_bias_kernel(tc, x, w4_words, w4_scales, down, up, b, out
             )
 
         def up_pass(i, acc):
-            c, m = i // TILES, (i % TILES) * P
+            c, m = i * P // UL, i * P % UL
             nc.tensor.matmul_mx(
-                out=acc[:],
+                out=acc,
                 lhsT=u_codes[c][:, m : m + P].bitcast(E4M3X4),
                 lhsT_scale=u_scales[c][:, m : m + P],
                 rhs=h_codes[:].bitcast(E4M3X4),
@@ -166,13 +173,13 @@ def tile_mix_lowrank_fm_bias_kernel(tc, x, w4_words, w4_scales, down, up, b, out
                 stop=(g == PASSES - 1),
             )
 
-        def finish(i, acc, on_vector):
+        def finish(i, acc, on_vector, ts=slice(0, T)):
             bias = b_cols[:, i : i + 1]
             if on_vector:
-                nc.vector.tensor_scalar(out=y_sb[i][:], in0=acc[:], scalar1=bias, scalar2=None, op0=ADD)
+                nc.vector.tensor_scalar(out=y_sb[i][:, ts], in0=acc, scalar1=bias, scalar2=None, op0=ADD)
             else:
-                nc.scalar.activation(out=y_sb[i][:], in_=acc[:], func=IDENTITY, bias=bias)
-            nc.sync.dma_start(out=out[i * P : (i + 1) * P, :], in_=y_sb[i][:])
+                nc.scalar.activation(out=y_sb[i][:, ts], in_=acc, func=IDENTITY, bias=bias)
+            nc.sync.dma_start(out=out[i * P : (i + 1) * P, ts], in_=y_sb[i][:, ts])
 
         nc.scalar.activation(out=warm[:], in_=warm[:], func=IDENTITY)
         b_psum = bank(7, "b_psum")
@@ -185,15 +192,15 @@ def tile_mix_lowrank_fm_bias_kernel(tc, x, w4_words, w4_scales, down, up, b, out
             interleave_both(x_bf[g], x_raw[g], X_SPLIT, T)
             if g == 0:
                 nc.scalar.copy(out=b_cols[:], in_=b_psum[:, 0:N_TILES])
-                for i in range(TILES):
+                for i in range(4):
                     acc[i] = bank(4 + i, f"y{i}")
             else:
                 quantize(d_codes[g - 1][:], d_scales[g - 1][:], d_bf[g - 1][:].rearrange("p t m j -> p (t m j)"))
                 for j in range(PACK):
                     h_pass(j, h_acc[j], g - 1)
             quantize_rows(x_codes[g], x_scales[g], x_bf[g])
-            for i in range(TILES):
-                w4_pass(i, acc[i], g)
+            for i in range(4):
+                w4_pass(i, acc[i][:], g)
             permute_both(g)
 
         last = PASSES - 1
@@ -207,42 +214,51 @@ def tile_mix_lowrank_fm_bias_kernel(tc, x, w4_words, w4_scales, down, up, b, out
             copy(out=h_sb[:, j, :], in_=h_acc[j][:])
         interleave_both(h_bf, h_sb, H_SPLIT, T)
         quantize_rows(h_codes, h_scales, h_bf)
-        interleave_both(u_bf[0], u_raw[0], UP_SPLIT, COLS)
-        quantize_rows(u_codes[0], u_scales[0], u_bf[0])
+
+        def quantize_up(c, lo, hi):
+            quantize(u_codes[c][:, lo:hi], u_scales[c][:, lo:hi], u_bf[c][:, lo:hi, :].rearrange("p w j -> p (w j)"))
+
+        def make_up(c):
+            interleave(nc.scalar.copy, u_bf[c], u_raw[c], UP_SPLIT, 512)
+            interleave(nc.vector.tensor_copy, u_bf[c], u_raw[c], 0, UP_SPLIT)
+            interleave(nc.scalar.copy, u_bf[c], u_raw[c], 640, UL)
+            interleave(nc.vector.tensor_copy, u_bf[c], u_raw[c], 512, 640)
+            quantize_up(c, 0, 512)
+            quantize_up(c, 512, UL)
 
         def w4_tile(i):
             acc[i] = bank(i - 4, f"y{i}")
             for g in range(PASSES):
-                w4_pass(i, acc[i], g)
+                w4_pass(i, acc[i][:], g)
 
-        for i in (4, 5, 6):
+        def up_tile(i):
+            up_pass(i, acc[i][:])
+
+        def out_tile(i, on_vector):
+            finish(i, acc[i][:], on_vector)
+
+        make_up(0)
+        for i in (4, 5, 6, 7):
             w4_tile(i)
-        for i in range(4):
-            up_pass(i, acc[i])
-        w4_tile(7)
-        finish(0, acc[0], False)
-        finish(1, acc[1], False)
-        interleave_both(u_bf[1], u_raw[1], UP_SPLIT, COLS)
-        finish(2, acc[2], False)
-        finish(3, acc[3], True)
-        quantize_rows(u_codes[1], u_scales[1], u_bf[1])
-        w4_tile(8)
-        for i in range(4, 8):
-            up_pass(i, acc[i])
-        finish(4, acc[4], False)
-        w4_tile(9)
-        finish(5, acc[5], False)
-        interleave_both(u_bf[2], u_raw[2], UP_SPLIT, COLS)
-        w4_tile(10)
-        finish(6, acc[6], False)
-        finish(7, acc[7], True)
-        quantize_rows(u_codes[2], u_scales[2], u_bf[2])
-        up_pass(8, acc[8])
-        finish(8, acc[8], False)
-        up_pass(9, acc[9])
-        finish(9, acc[9], True)
+        for i in range(6):
+            up_tile(i)
+        out_tile(0, False)
+        out_tile(1, True)
+        out_tile(2, False)
+        out_tile(3, True)
+        out_tile(4, False)
+        out_tile(5, True)
+        for i in (8, 9, 10):
+            w4_tile(i)
+        make_up(1)
+        for i in (6, 7, 8, 9, 10):
+            up_tile(i)
+        out_tile(6, False)
+        out_tile(7, True)
+        out_tile(8, False)
+        out_tile(9, True)
+        out_tile(10, False)
         w4_tile(11)
-        up_pass(10, acc[10])
-        finish(10, acc[10], False)
-        up_pass(11, acc[11])
-        finish(11, acc[11], True)
+        up_tile(11)
+        finish(11, acc[11][:, 0 : T // 2], True, slice(0, T // 2))
+        finish(11, acc[11][:, T // 2 : T], True, slice(T // 2, T))

@@ -194,21 +194,19 @@ def tile_mix_lowrank_fm_bias_kernel(tc, x, w4_words, w4_scales, down, up, b, out
                 nc.scalar.copy(out=b_cols[:], in_=b_psum[:, 0:N_TILES])
                 for i in range(4):
                     acc[i] = bank(4 + i, f"y{i}")
-            else:
-                quantize(d_codes[g - 1][:], d_scales[g - 1][:], d_bf[g - 1][:].rearrange("p t m j -> p (t m j)"))
-                for j in range(PACK):
-                    h_pass(j, h_acc[j], g - 1)
             quantize_rows(x_codes[g], x_scales[g], x_bf[g])
             for i in range(4):
                 w4_pass(i, acc[i][:], g)
             permute_both(g)
+            if g < PASSES - 1:
+                quantize(d_codes[g][:], d_scales[g][:], d_bf[g][:].rearrange("p t m j -> p (t m j)"))
+            else:
+                for j in range(PACK):
+                    cols = slice(j * P, (j + 1) * P)
+                    quantize(d_codes[g][:, cols], d_scales[g][:, cols], d_bf[g][:, j, :, :].rearrange("p m j -> p (m j)"))
+            for j in range(PACK):
+                h_pass(j, h_acc[j], g)
 
-        last = PASSES - 1
-        for j in range(PACK):
-            cols = slice(j * P, (j + 1) * P)
-            quantize(d_codes[last][:, cols], d_scales[last][:, cols], d_bf[last][:, j, :, :].rearrange("p m j -> p (m j)"))
-        for j in range(PACK):
-            h_pass(j, h_acc[j], last)
         for j in range(PACK):
             copy = nc.vector.tensor_copy if j % 2 else nc.scalar.copy
             copy(out=h_sb[:, j, :], in_=h_acc[j][:])

from contextlib import ExitStack

import concourse.mybir as mybir
from concourse.masks import make_identity

K, R, N, T = 2048, 512, 1536, 512
FLOPS = 2 * T * (K * R + K * N + R * N)

F32 = mybir.dt.float32
BF16 = mybir.dt.bfloat16
I32 = mybir.dt.int32
U32 = mybir.dt.uint32
U8 = mybir.dt.uint8
E4M3X4 = mybir.dt.float8_e4m3fn_x4
E2M1X4 = mybir.dt.float4_e2m1fn_x4
IDENTITY = mybir.ActivationFunctionType.Identity
ADD = mybir.AluOpType.add

P = 128
PACK = 4
K_PASS = P * PACK
PASSES = K // K_PASS
N_TILES = N // P
W_COLS = (512, 1024)
W_LOADS = 3
U_LOADS = 2
WL = N // W_LOADS
UL = N // U_LOADS

X_SPLIT = 352
DOWN_SPLIT = 88
UP_SPLIT = 384
H_SPLIT = 352


def tile_mix_lowrank_fm_bias_kernel(tc, x, w4_words, w4_scales, down, up, b, out):
    nc = tc.nc
    with ExitStack() as ctx:
        keep = ctx.enter_context(tc.tile_pool(name="keep", bufs=1))
        psum = ctx.enter_context(tc.psum_pool(name="psum", bufs=1))
        ctx.enter_context(tc.manual_schedule())

        def sbuf(name, shape, dtype):
            return keep.tile(shape, dtype, name=name, align_bytes=64)

        def bank(i, name):
            return psum.tile([P, T], F32, name=name, tag=f"bank{i}")

        x_raw = [sbuf(f"x_raw{g}", [P, PACK, T], F32) for g in range(PASSES)]
        x_bf = [sbuf(f"x_bf{g}", [P, T, PACK], BF16) for g in range(PASSES)]
        x_codes = [sbuf(f"x_codes{g}", [P, T], U32) for g in range(PASSES)]
        x_scales = [sbuf(f"x_scales{g}", [P, T], U8) for g in range(PASSES)]
        d_raw = [sbuf(f"d_raw{g}", [P, PACK, R], F32) for g in range(PASSES)]
        d_bf = [sbuf(f"d_bf{g}", [P, PACK, P, PACK], BF16) for g in range(PASSES)]
        d_codes = [sbuf(f"d_codes{g}", [P, R], U32) for g in range(PASSES)]
        d_scales = [sbuf(f"d_scales{g}", [P, R], U8) for g in range(PASSES)]
        u_raw = [sbuf(f"u_raw{c}", [P, PACK, UL], F32) for c in range(U_LOADS)]
        u_bf = [sbuf(f"u_bf{c}", [P, UL, PACK], BF16) for c in range(U_LOADS)]
        u_codes = [sbuf(f"u_codes{c}", [P, UL], U32) for c in range(U_LOADS)]
        u_scales = [sbuf(f"u_scales{c}", [P, UL], U8) for c in range(U_LOADS)]
        w_words = [sbuf(f"w_words{c}", [P, PASSES, 2 * WL], U8) for c in range(W_LOADS)]
        w_scales = [sbuf(f"w_scales{c}", [P, PASSES, n], U8) for c, n in enumerate(W_COLS)]
        h_sb = sbuf("h_sb", [P, PACK, T], BF16)
        h_bf = sbuf("h_bf", [P, T, PACK], BF16)
        h_codes = sbuf("h_codes", [P, T], U32)
        h_scales = sbuf("h_scales", [P, T], U8)
        ident = sbuf("ident", [P, P], F32)
        b_rows = sbuf("b_rows", [P, P], F32)
        b_cols = sbuf("b_cols", [P, N_TILES], F32)
        warm = sbuf("warm", [P, 1], F32)
        y_sb = [sbuf(f"y_sb{i}", [P, T], F32) for i in range(N_TILES)]

        nc.vector.memset(warm[:], 0.0)
        nc.vector.memset(b_rows[:], 0.0)
        for c in range(2):
            nc.vector.memset(w_scales[c][:].rearrange("p g n -> p (g n)").bitcast(I32), 0)
        make_identity(nc, ident[:])

        def load_rows(tile, rows):
            nc.sync.dma_start(out=tile[:], in_=rows.rearrange("(p j) w -> p j w", j=PACK))

        def load_w_words(c):
            nc.sync.dma_start(
                out=w_words[c][:],
                in_=w4_words[:, :, 2 * c * WL : 2 * (c + 1) * WL].rearrange("g p n -> p g n"),
            )

        def load_w_scales(c):
            cols = slice(sum(W_COLS[:c]), sum(W_COLS[: c + 1]))
            for r in range(4):
                nc.sync.dma_start(
                    out=w_scales[c][r:P:32, :, :].bitcast(I32),
                    in_=w4_scales[:, r:16:4, cols].rearrange("g q n -> q g n").bitcast(I32),
                )

        nc.scalar.dma_start(out=b_rows[0:N_TILES, :], in_=b.rearrange("(c p) -> c p", p=P))
        k_rows = [slice(g * K_PASS, (g + 1) * K_PASS) for g in range(PASSES)]
        u_cols = [slice(c * UL, (c + 1) * UL) for c in range(U_LOADS)]
        load_rows(x_raw[0], x[k_rows[0], :])
        load_rows(d_raw[0], down[k_rows[0], :])
        load_w_words(0)
        load_w_scales(0)
        for g in range(1, PASSES):
            load_rows(x_raw[g], x[k_rows[g], :])
            load_rows(d_raw[g], down[k_rows[g], :])
        load_w_words(1)
        load_w_scales(1)
        load_rows(u_raw[0], up[:, u_cols[0]])
        load_w_words(2)
        load_rows(u_raw[1], up[:, u_cols[1]])

        def interleave(copy, dst, src, lo, hi):
            copy(
                out=dst[:, lo:hi, :].rearrange("p (c i) t -> p c t i", i=4),
                in_=src[:, :, lo:hi].rearrange("p t (c i) -> p c t i", i=4),
            )

        def interleave_both(dst, src, split, width):
            interleave(nc.vector.tensor_copy, dst, src, 0, split)
            interleave(nc.scalar.copy, dst, src, split, width)

        def permute(copy, g, lo, hi):
            for t in (0, 2):
                copy(
                    out=d_bf[g][:, t : t + 2, lo:hi, :].rearrange("p t m j -> p m j t"),
                    in_=d_raw[g][:, :, 4 * lo : 4 * hi].rearrange("p j (m t) -> p m j t", t=4)[:, :, :, t : t + 2],
                )

        def permute_both(g):
            permute(nc.vector.tensor_copy, g, 0, DOWN_SPLIT)
            permute(nc.scalar.copy, g, DOWN_SPLIT, P)

        def quantize(codes, scales, grouped):
            nc.vector.quantize_mx(out=codes.bitcast(E4M3X4), scales=scales, in_=grouped)

        def quantize_rows(codes, scales, grouped):
            quantize(codes[:], scales[:], grouped[:].rearrange("p w j -> p (w j)"))

        def w4_pass(i, acc, g):
            c, m = i * P // WL, i * P % WL
            d, n = (0, i * P) if i * P < W_COLS[0] else (1, i * P - W_COLS[0])
            nc.tensor.matmul_mx(
                out=acc,
                lhsT=w_words[c][:, g, 2 * m : 2 * (m + P)].bitcast(E2M1X4),
                lhsT_scale=w_scales[d][:, g, n : n + P],
                rhs=x_codes[g][:].bitcast(E4M3X4),
                rhs_scale=x_scales[g][:],
                start=(g == 0),
                stop=False,
            )

        def up_pass(i, acc):
            c, m = i * P // UL, i * P % UL
            nc.tensor.matmul_mx(
                out=acc,
                lhsT=u_codes[c][:, m : m + P].bitcast(E4M3X4),
                lhsT_scale=u_scales[c][:, m : m + P],
                rhs=h_codes[:].bitcast(E4M3X4),
                rhs_scale=h_scales[:],
                start=False,
                stop=True,
            )

        def h_pass(j, acc, g):
            cols = slice(j * P, (j + 1) * P)
            nc.tensor.matmul_mx(
                out=acc[:],
                lhsT=d_codes[g][:, cols].bitcast(E4M3X4),
                lhsT_scale=d_scales[g][:, cols],
                rhs=x_codes[g][:].bitcast(E4M3X4),
                rhs_scale=x_scales[g][:],
                start=(g == 0),
                stop=(g == PASSES - 1),
            )

        def finish(i, acc, on_vector, ts=slice(0, T)):
            bias = b_cols[:, i : i + 1]
            if on_vector:
                nc.vector.tensor_scalar(out=y_sb[i][:, ts], in0=acc, scalar1=bias, scalar2=None, op0=ADD)
            else:
                nc.scalar.activation(out=y_sb[i][:, ts], in_=acc, func=IDENTITY, bias=bias)
            nc.sync.dma_start(out=out[i * P : (i + 1) * P, ts], in_=y_sb[i][:, ts])

        nc.scalar.activation(out=warm[:], in_=warm[:], func=IDENTITY)
        b_psum = bank(7, "b_psum")
        nc.tensor.transpose(b_psum[:, 0:P], b_rows[:], ident[:])

        acc = {}
        h_acc = [bank(j, f"h{j}") for j in range(PACK)]

        for g in range(PASSES):
            interleave_both(x_bf[g], x_raw[g], X_SPLIT, T)
            if g == 0:
                nc.scalar.copy(out=b_cols[:], in_=b_psum[:, 0:N_TILES])
                for i in range(4):
                    acc[i] = bank(4 + i, f"y{i}")
            quantize_rows(x_codes[g], x_scales[g], x_bf[g])
            for i in range(4):
                w4_pass(i, acc[i][:], g)
            permute_both(g)
            if g < PASSES - 1:
                quantize(d_codes[g][:], d_scales[g][:], d_bf[g][:].rearrange("p t m j -> p (t m j)"))
            else:
                for j in range(PACK):
                    cols = slice(j * P, (j + 1) * P)
                    quantize(d_codes[g][:, cols], d_scales[g][:, cols], d_bf[g][:, j, :, :].rearrange("p m j -> p (m j)"))
            for j in range(PACK):
                h_pass(j, h_acc[j], g)

        for j in range(PACK):
            copy = nc.vector.tensor_copy if j % 2 else nc.scalar.copy
            copy(out=h_sb[:, j, :], in_=h_acc[j][:])
        interleave_both(h_bf, h_sb, H_SPLIT, T)
        quantize_rows(h_codes, h_scales, h_bf)

        def quantize_up(c, lo, hi):
            quantize(u_codes[c][:, lo:hi], u_scales[c][:, lo:hi], u_bf[c][:, lo:hi, :].rearrange("p w j -> p (w j)"))

        def make_up(c):
            interleave(nc.scalar.copy, u_bf[c], u_raw[c], UP_SPLIT, 512)
            interleave(nc.vector.tensor_copy, u_bf[c], u_raw[c], 0, UP_SPLIT)
            interleave(nc.scalar.copy, u_bf[c], u_raw[c], 640, UL)
            interleave(nc.vector.tensor_copy, u_bf[c], u_raw[c], 512, 640)
            quantize_up(c, 0, 512)
            quantize_up(c, 512, UL)

        def w4_tile(i):
            acc[i] = bank(i - 4, f"y{i}")
            for g in range(PASSES):
                w4_pass(i, acc[i][:], g)

        def up_tile(i):
            up_pass(i, acc[i][:])

        def out_tile(i, on_vector):
            finish(i, acc[i][:], on_vector)

        make_up(0)
        for i in (4, 5, 6, 7):
            w4_tile(i)
        for i in range(6):
            up_tile(i)
        out_tile(0, False)
        out_tile(1, True)
        out_tile(2, False)
        out_tile(3, True)
        out_tile(4, False)
        out_tile(5, True)
        for i in (8, 9, 10):
            w4_tile(i)
        make_up(1)
        for i in (6, 7, 8, 9, 10):
            up_tile(i)
        out_tile(6, False)
        out_tile(7, True)
        out_tile(8, False)
        out_tile(9, True)
        out_tile(10, False)
        w4_tile(11)
        up_tile(11)
        finish(11, acc[11][:, 0 : T // 2], True, slice(0, T // 2))
        finish(11, acc[11][:, T // 2 : T], True, slice(T // 2, T))
